import numpy as np
import ml_dtypes


def mxq(x, axis, fmt="e4m3"):
    dtype, down = {"e4m3": (ml_dtypes.float8_e4m3fn, 7), "e5m2": (ml_dtypes.float8_e5m2, 14)}[fmt]
    v = np.moveaxis(np.asarray(x, np.float32).astype(ml_dtypes.bfloat16).astype(np.float64), axis, -1)
    blocks = v.reshape(v.shape[:-1] + (-1, 32))
    amax = np.abs(blocks).max(-1, keepdims=True)
    byte = np.maximum(np.where(amax > 0, np.frexp(amax)[1] - 1 + 127, 0) - down, 1)
    scale = np.exp2(byte - 127.0)
    codes = (blocks / scale).astype(np.float32).astype(dtype).astype(np.float64)
    return np.moveaxis((codes * scale).reshape(v.shape), -1, axis)


WIDE = False


def mx_kscale(k):
    if not WIDE:
        return np.ones(k)
    levels = np.array([10, -10, 5, -5, 0])
    if k % 512:
        return np.exp2(np.random.permutation(np.resize(levels, k // 32))).repeat(32)
    a = np.empty((k // 512, 16))
    for p in range(k // 512):
        a[p, :8] = np.random.permutation(np.resize(levels, 8))
        for g in range(8):
            far = levels[np.abs(levels - a[p, g]) >= 10]
            a[p, g + 8] = far[np.random.randint(len(far))]
    return np.exp2(a.ravel()).repeat(32)


def f64(x):
    return np.asarray(x).astype(np.float64)


def striped(idx):
    return np.tile(idx.reshape(-1, 16).T, (8, 1)).astype(np.uint16)


def unstriped(offs):
    return offs[:16].T.reshape(-1).astype(np.int64)


K, T, E, C, N = 2560, 1024, 6, 128, 128


def by_expert(wq, xq):
    return np.concatenate([wq[e].T @ xq[:, e * C:(e + 1) * C] for e in range(E)], axis=1)


def setup_inputs():
    n = np.random.standard_normal
    s = mx_kscale(K)[:, None]
    return {
        "xT": (n((K, T)) * s).astype(np.float32),
        "w": (n((E, K, N)) / np.sqrt(K) / s[None]).astype(np.float32),
        "b": (0.3 * n((N, E))).astype(np.float32),
        "gate": np.tile(np.random.uniform(0.2, 1.0, E * C), (K, 1)).astype(np.float32),
        "offs": striped(np.random.permutation(T)[:E * C]),
    }


def reference(xT, w, b, gate, offs):
    idx = unstriped(offs)
    xq = mxq(f64(gate) * f64(xT)[:, idx], 0, "e4m3")
    y = by_expert(mxq(f64(w), 1, "e4m3"), xq)
    y = y + np.repeat(f64(b), C, axis=1)
    out = np.zeros((N, T))
    out[:, idx] = y
    return out

@@ -1,0 +1,208 @@
+from contextlib import ExitStack
+
+import concourse.mybir as mybir
+
+K, T, E, C, N = 2560, 1024, 6, 128, 128
+S = E * C
+FLOPS = 2 * K * N * S
+BYTES = 4 * (K * T + E * K * N + N * E + 128 * S + N * T) + 2 * 128 * (S // 16)
+
+F32 = mybir.dt.float32
+BF16 = mybir.dt.bfloat16
+U32 = mybir.dt.uint32
+U16 = mybir.dt.uint16
+U8 = mybir.dt.uint8
+FP8X4 = mybir.dt.float8_e4m3fn_x4
+MULT = mybir.AluOpType.mult
+IDENT = mybir.ActivationFunctionType.Identity
+
+P = 128
+PACK = 4
+K_PASS = P * PACK
+PASSES = K // K_PASS
+GROUPS = 3
+GE = E // GROUPS
+GS = GE * C
+LINE = 4
+
+
+def tile_moe_pre_lin_bias_kernel(tc, xT, w, b, gate, offs, out):
+    nc = tc.nc
+    with ExitStack() as ctx:
+        keep = ctx.enter_context(tc.tile_pool(name="keep", bufs=1))
+        ring = ctx.enter_context(tc.tile_pool(name="ring", bufs=3))
+        psum = ctx.enter_context(tc.psum_pool(name="psum", bufs=1))
+
+        offsets = keep.tile([P, S // 16], U16, name="offsets")
+        gate_sb = keep.tile([P, S], F32, name="gate_sb")
+        bias = keep.tile([P, E], F32, name="bias")
+        window = keep.tile([P, T], F32, name="window")
+        x_raw = {}
+        w_raw = {}
+
+        def load_x(g, t):
+            x_raw[g, t] = ring.tile([P, T], F32, name="x_raw", bufs=14)
+            rows = xT[g * K_PASS : (g + 1) * K_PASS, :].rearrange("(p j) c -> p j c", j=PACK)
+            nc.sync.dma_start(out=x_raw[g, t][:], in_=rows[:, t, :])
+
+        def load_w(g, h):
+            w_raw[g, h] = keep.tile([P, GE, PACK, N], F32, name="w_raw_%d_%d" % (g, h))
+            rows = w[h * GE : (h + 1) * GE, g * K_PASS : (g + 1) * K_PASS, :]
+            nc.sync.dma_start(
+                out=w_raw[g, h][:].rearrange("p e j n -> p e (j n)"),
+                in_=rows.rearrange("e (p j) n -> p e (j n)", j=PACK),
+            )
+
+        nc.sync.dma_start(offsets[:], offs)
+        nc.sync.dma_start(out=gate_sb[:], in_=gate[0:P, :])
+        order = "xxxwxxwxxwxbwwxwxxwxwwxxwxxxxxxwwwww"
+        xs = [(g, t) for g in range(PASSES) for t in range(PACK)]
+        ws = [(g, h) for g in range(3) for h in range(GROUPS)] + [(g, h) for h in range(GROUPS) for g in (3, 4)]
+        xi = 0
+        wi = 0
+        for kind in order:
+            if kind == "x":
+                load_x(*xs[xi])
+                xi += 1
+            elif kind == "w":
+                load_w(*ws[wi])
+                wi += 1
+            else:
+                nc.sync.dma_start(out=bias[:], in_=b)
+        nc.vector.memset(window[:], 0.0)
+
+        acc = [psum.tile([N, 512], F32, name="acc_%d" % e) for e in range(E)]
+        gathered = {}
+        x_bf = {}
+        w_bf = {}
+        x_q = {}
+        w_q = {}
+
+        def gather_whole(g):
+            g4 = ring.tile([P, PACK, S], F32, name="g4", bufs=2)
+            for t in range(PACK):
+                nc.vector.tensor_tensor(g4[:, t, :], x_raw[g, t][:].indirect(offsets[:]), gate_sb[:], MULT)
+            gathered[g] = g4[:]
+
+        def gather_group(g, h):
+            part = ring.tile([P, PACK, GS], F32, name="part")
+            cols = offsets[:, h * GS // 16 : (h + 1) * GS // 16]
+            for t in range(PACK):
+                nc.vector.tensor_tensor(
+                    part[:, t, :], x_raw[g, t][:].indirect(cols), gate_sb[:, h * GS : (h + 1) * GS], MULT
+                )
+            gathered[g, h] = part[:]
+
+        def interleave(dst, src):
+            nc.scalar.copy(
+                out=dst.rearrange("p (c i t) -> p c t i", i=LINE, t=PACK),
+                in_=src.rearrange("p t (c i) -> p c t i", i=LINE),
+            )
+
+        def round_x(g, h):
+            x_bf[g, h] = ring.tile([P, GS * PACK], BF16, name="x_bf", bufs=3, align_bytes=64)
+            interleave(x_bf[g, h][:], gathered[g, h])
+
+        def round_x_whole(g):
+            x_bf[g] = ring.tile([P, S * PACK], BF16, name="x_bf_whole", bufs=2, align_bytes=64)
+            interleave(x_bf[g][:], gathered[g])
+
+        def round_w(g, h):
+            w_bf[g, h] = ring.tile([P, GE * N * PACK], BF16, name="w_bf", bufs=6, align_bytes=64)
+            for i in range(GE):
+                interleave(w_bf[g, h][:, i * N * PACK : (i + 1) * N * PACK], w_raw[g, h][:, i, :, :])
+
+        def quantize(src, name):
+            width = src.shape[1] // PACK
+            codes = keep.tile([P, width], U32, name=name + "_codes", align_bytes=64)
+            scales = keep.tile([P, width], U8, name=name + "_scales", align_bytes=64)
+            for a in range(0, width, 512):
+                z = min(a + 512, width)
+                nc.vector.quantize_mx(
+                    out=codes[:, a:z].bitcast(FP8X4), scales=scales[:, a:z], in_=src[:, a * PACK : z * PACK]
+                )
+            return codes, scales
+
+        def quantize_x_whole(g):
+            codes, scales = quantize(x_bf[g], "x_%d" % g)
+            for h in range(GROUPS):
+                x_q[g, h] = codes[:, h * GS : (h + 1) * GS], scales[:, h * GS : (h + 1) * GS]
+
+        def quantize_x(g, h):
+            x_q[g, h] = quantize(x_bf[g, h], "x_%d_%d" % (g, h))
+
+        def quantize_w(g, h):
+            w_q[g, h] = quantize(w_bf[g, h], "w_%d_%d" % (g, h))
+
+        def multiply(g, h):
+            w_codes, w_scales = w_q[g, h]
+            x_codes, x_scales = x_q[g, h]
+            for i in range(GE):
+                nc.tensor.matmul_mx(
+                    out=acc[h * GE + i][:, 0:C],
+                    lhsT=w_codes[:, i * N : (i + 1) * N].bitcast(FP8X4),
+                    lhsT_scale=w_scales[:, i * N : (i + 1) * N],
+                    rhs=x_codes[:, i * C : (i + 1) * C].bitcast(FP8X4),
+                    rhs_scale=x_scales[:, i * C : (i + 1) * C],
+                    start=(g == 0),
+                    stop=(g == PASSES - 1),
+                )
+
+        sums = {}
+
+        def add_bias(h):
+            sums[h] = keep.tile([P, GS], F32, name="y_%d" % h)
+            for i in range(GE):
+                e = h * GE + i
+                nc.scalar.activation(sums[h][:, i * C : (i + 1) * C], acc[e][:, 0:C], IDENT, bias=bias[:, e : e + 1])
+
+        def scatter(h):
+            cols = offsets[:, h * GS // 16 : (h + 1) * GS // 16]
+            nc.vector.tensor_copy(window[:].indirect(cols), sums[h][:])
+
+        gather_whole(0)
+        for g in range(3):
+            for h in range(GROUPS):
+                round_w(g, h)
+            round_x_whole(g)
+            gather_whole(g + 1)
+            quantize_x_whole(g)
+            for h in range(GROUPS):
+                quantize_w(g, h)
+                multiply(g, h)
+        round_w(3, 0)
+        round_x_whole(3)
+        gather_group(4, 0)
+        round_w(4, 0)
+        round_x(4, 0)
+        quantize_x_whole(3)
+        quantize_w(3, 0)
+        multiply(3, 0)
+        gather_group(4, 1)
+        round_w(3, 1)
+        round_w(4, 1)
+        round_x(4, 1)
+        quantize_w(4, 0)
+        quantize_x(4, 0)
+        multiply(4, 0)
+        gather_group(4, 2)
+        round_w(3, 2)
+        add_bias(0)
+        round_w(4, 2)
+        round_x(4, 2)
+        quantize_w(3, 1)
+        quantize_w(4, 1)
+        quantize_x(4, 1)
+        multiply(3, 1)
+        multiply(4, 1)
+        add_bias(1)
+        scatter(0)
+        quantize_w(3, 2)
+        quantize_w(4, 2)
+        quantize_x(4, 2)
+        multiply(3, 2)
+        multiply(4, 2)
+        add_bias(2)
+        scatter(1)
+        scatter(2)
+        nc.sync.dma_start(out=out, in_=window[:])

@@ -3,9 +3,10 @@ from contextlib import ExitStack
 import concourse.mybir as mybir
 
 K, T, E, C, N = 2560, 1024, 6, 128, 128
-S = E * C
-FLOPS = 2 * K * N * S
-BYTES = 4 * (K * T + E * K * N + N * E + 128 * S + N * T) + 2 * 128 * (S // 16)
+SLOTS = E * C
+P = 128
+FLOPS = 2 * K * N * SLOTS
+BYTES = 4 * (K * T + E * K * N + N * E + P * SLOTS + N * T) + 2 * P * (SLOTS // 16)
 
 F32 = mybir.dt.float32
 BF16 = mybir.dt.bfloat16
@@ -14,29 +15,36 @@ U16 = mybir.dt.uint16
 U8 = mybir.dt.uint8
 FP8X4 = mybir.dt.float8_e4m3fn_x4
 MULT = mybir.AluOpType.mult
-IDENT = mybir.ActivationFunctionType.Identity
+IDENTITY = mybir.ActivationFunctionType.Identity
 
-P = 128
 PACK = 4
 K_PASS = P * PACK
 PASSES = K // K_PASS
-GROUPS = 3
-GE = E // GROUPS
-GS = GE * C
-LINE = 4
+LAST = PASSES - 1
+PER_COLUMN = 16
+BANK = 512
+QUANT_WORDS = 512
+RUN = 2
+GROUPS = ((0, 2), (2, 4), (4, 6))
+FIRST = 256
+SPLIT = 4
 
 
 def tile_moe_pre_lin_bias_kernel(tc, xT, w, b, gate, offs, out):
     nc = tc.nc
     with ExitStack() as ctx:
         keep = ctx.enter_context(tc.tile_pool(name="keep", bufs=1))
-        ring = ctx.enter_context(tc.tile_pool(name="ring", bufs=3))
+        ring = ctx.enter_context(tc.tile_pool(name="ring", bufs=2))
         psum = ctx.enter_context(tc.psum_pool(name="psum", bufs=1))
 
-        offsets = keep.tile([P, S // 16], U16, name="offsets")
-        gate_sb = keep.tile([P, S], F32, name="gate_sb")
+        offsets = keep.tile([P, SLOTS // PER_COLUMN], U16, name="offsets")
+        gate_sb = keep.tile([P, SLOTS], F32, name="gate_sb")
         bias = keep.tile([P, E], F32, name="bias")
         window = keep.tile([P, T], F32, name="window")
+
+        batches = [[(e, LAST) for e in range(SPLIT, E)]]
+        batches += [[(e, g) for g in range(LAST)] for e in range(E)]
+        batches += [[(e, LAST) for e in range(SPLIT)]]
         x_raw = {}
         w_raw = {}
 
@@ -45,164 +53,135 @@ def tile_moe_pre_lin_bias_kernel(tc, xT, w, b, gate, offs, out):
             rows = xT[g * K_PASS : (g + 1) * K_PASS, :].rearrange("(p j) c -> p j c", j=PACK)
             nc.sync.dma_start(out=x_raw[g, t][:], in_=rows[:, t, :])
 
-        def load_w(g, h):
-            w_raw[g, h] = keep.tile([P, GE, PACK, N], F32, name="w_raw_%d_%d" % (g, h))
-            rows = w[h * GE : (h + 1) * GE, g * K_PASS : (g + 1) * K_PASS, :]
-            nc.sync.dma_start(
-                out=w_raw[g, h][:].rearrange("p e j n -> p e (j n)"),
-                in_=rows.rearrange("e (p j) n -> p e (j n)", j=PACK),
-            )
-
-        nc.sync.dma_start(offsets[:], offs)
-        nc.sync.dma_start(out=gate_sb[:], in_=gate[0:P, :])
-        order = "xxxwxxwxxwxbwwxwxxwxwwxxwxxxxxxwwwww"
-        xs = [(g, t) for g in range(PASSES) for t in range(PACK)]
-        ws = [(g, h) for g in range(3) for h in range(GROUPS)] + [(g, h) for h in range(GROUPS) for g in (3, 4)]
-        xi = 0
-        wi = 0
-        for kind in order:
-            if kind == "x":
-                load_x(*xs[xi])
-                xi += 1
-            elif kind == "w":
-                load_w(*ws[wi])
-                wi += 1
+        def load_w(i):
+            (e0, g0), (e1, g1) = batches[i][0], batches[i][-1]
+            w_raw[i] = keep.tile([P, len(batches[i]), PACK * N], F32, name="w_raw_%d" % i)
+            rows = w[e0 : e1 + 1, g0 * K_PASS : (g1 + 1) * K_PASS, :]
+            if e0 == e1:
+                src = rows[0].rearrange("(g p j) n -> p g (j n)", p=P, j=PACK)
             else:
+                src = rows.rearrange("e (p j) n -> p e (j n)", j=PACK)
+            nc.sync.dma_start(out=w_raw[i][:], in_=src)
+
+        with_pass = [[0], [1, 2], [3, 4], [5, 6], [7]]
+        for g in range(PASSES):
+            for t in range(PACK - 1):
+                load_x(g, t)
+                if (g, t) == (0, 0):
+                    nc.sync.dma_start(offsets[:], offs)
+                    nc.sync.dma_start(out=gate_sb[:, 0:FIRST], in_=gate[0:P, 0:FIRST])
+                    nc.sync.dma_start(out=gate_sb[:, FIRST:SLOTS], in_=gate[0:P, FIRST:SLOTS])
+            for i in with_pass[g]:
+                load_w(i)
+            if g == 1:
                 nc.sync.dma_start(out=bias[:], in_=b)
+            load_x(g, PACK - 1)
         nc.vector.memset(window[:], 0.0)
 
-        acc = [psum.tile([N, 512], F32, name="acc_%d" % e) for e in range(E)]
-        gathered = {}
-        x_bf = {}
-        w_bf = {}
+        acc = [psum.tile([N, BANK], F32, name="acc_%d" % e) for e in range(E)]
+        planes = {}
         x_q = {}
         w_q = {}
+        done = set()
 
-        def gather_whole(g):
-            g4 = ring.tile([P, PACK, S], F32, name="g4", bufs=2)
-            for t in range(PACK):
-                nc.vector.tensor_tensor(g4[:, t, :], x_raw[g, t][:].indirect(offsets[:]), gate_sb[:], MULT)
-            gathered[g] = g4[:]
+        def listed(a, z):
+            return offsets[:, a // PER_COLUMN : z // PER_COLUMN]
 
-        def gather_group(g, h):
-            part = ring.tile([P, PACK, GS], F32, name="part")
-            cols = offsets[:, h * GS // 16 : (h + 1) * GS // 16]
+        def gather(g):
+            planes[g] = ring.tile([P, PACK, SLOTS], F32, name="planes")
             for t in range(PACK):
-                nc.vector.tensor_tensor(
-                    part[:, t, :], x_raw[g, t][:].indirect(cols), gate_sb[:, h * GS : (h + 1) * GS], MULT
-                )
-            gathered[g, h] = part[:]
+                if (g, t) == (0, 0):
+                    cuts = [(0, FIRST), (FIRST, SLOTS)]
+                elif (g, t) == (LAST, PACK - 1):
+                    cuts = [(e0 * C, e1 * C) for e0, e1 in GROUPS]
+                else:
+                    cuts = [(0, SLOTS)]
+                for a, z in cuts:
+                    nc.vector.tensor_tensor(
+                        planes[g][:, t, a:z], x_raw[g, t][:].indirect(listed(a, z)), gate_sb[:, a:z], MULT
+                    )
 
         def interleave(dst, src):
             nc.scalar.copy(
-                out=dst.rearrange("p (c i t) -> p c t i", i=LINE, t=PACK),
-                in_=src.rearrange("p t (c i) -> p c t i", i=LINE),
+                out=dst.rearrange("p (c i t) -> p c t i", i=RUN, t=PACK),
+                in_=src.rearrange("p t (c i) -> p c t i", i=RUN),
             )
 
-        def round_x(g, h):
-            x_bf[g, h] = ring.tile([P, GS * PACK], BF16, name="x_bf", bufs=3, align_bytes=64)
-            interleave(x_bf[g, h][:], gathered[g, h])
+        def round_x(g, e0, e1, tag, bufs):
+            rounded = ring.tile([P, (e1 - e0) * C * PACK], BF16, name=tag, bufs=bufs, align_bytes=64)
+            interleave(rounded[:], planes[g][:, :, e0 * C : e1 * C])
+            return rounded
 
-        def round_x_whole(g):
-            x_bf[g] = ring.tile([P, S * PACK], BF16, name="x_bf_whole", bufs=2, align_bytes=64)
-            interleave(x_bf[g][:], gathered[g])
+        def round_w(i):
+            rounded = ring.tile([P, len(batches[i]) * N * PACK], BF16, name="w_bf", bufs=3, align_bytes=64)
+            for u in range(len(batches[i])):
+                src = w_raw[i][:, u, :].rearrange("p (t n) -> p t n", t=PACK)
+                interleave(rounded[:, u * N * PACK : (u + 1) * N * PACK], src)
+            return rounded
 
-        def round_w(g, h):
-            w_bf[g, h] = ring.tile([P, GE * N * PACK], BF16, name="w_bf", bufs=6, align_bytes=64)
-            for i in range(GE):
-                interleave(w_bf[g, h][:, i * N * PACK : (i + 1) * N * PACK], w_raw[g, h][:, i, :, :])
-
-        def quantize(src, name):
-            width = src.shape[1] // PACK
+        def quantize(rounded, name, store, keys):
+            width = rounded.shape[1] // PACK
             codes = keep.tile([P, width], U32, name=name + "_codes", align_bytes=64)
             scales = keep.tile([P, width], U8, name=name + "_scales", align_bytes=64)
-            for a in range(0, width, 512):
-                z = min(a + 512, width)
+            for a in range(0, width, QUANT_WORDS):
+                z = min(a + QUANT_WORDS, width)
                 nc.vector.quantize_mx(
-                    out=codes[:, a:z].bitcast(FP8X4), scales=scales[:, a:z], in_=src[:, a * PACK : z * PACK]
+                    out=codes[:, a:z].bitcast(FP8X4), scales=scales[:, a:z], in_=rounded[:, a * PACK : z * PACK]
                 )
-            return codes, scales
+            for u, key in enumerate(keys):
+                store[key] = codes[:, u * P : (u + 1) * P].bitcast(FP8X4), scales[:, u * P : (u + 1) * P]
 
-        def quantize_x_whole(g):
-            codes, scales = quantize(x_bf[g], "x_%d" % g)
-            for h in range(GROUPS):
-                x_q[g, h] = codes[:, h * GS : (h + 1) * GS], scales[:, h * GS : (h + 1) * GS]
+        def multiply():
+            for g in range(PASSES):
+                for e in range(E):
+                    ready = (e, g) in x_q and (e, g) in w_q and (g == 0 or (e, g - 1) in done)
+                    if ready and (e, g) not in done:
+                        nc.tensor.matmul_mx(
+                            out=acc[e][:, 0:C],
+                            lhsT=w_q[e, g][0],
+                            lhsT_scale=w_q[e, g][1],
+                            rhs=x_q[e, g][0],
+                            rhs_scale=x_q[e, g][1],
+                            start=(g == 0),
+                            stop=(g == LAST),
+                        )
+                        done.add((e, g))
 
-        def quantize_x(g, h):
-            x_q[g, h] = quantize(x_bf[g, h], "x_%d_%d" % (g, h))
+        def prepare_w(g):
+            for i in with_pass[g]:
+                quantize(round_w(i), "w_%d" % i, w_q, batches[i])
 
-        def quantize_w(g, h):
-            w_q[g, h] = quantize(w_bf[g, h], "w_%d_%d" % (g, h))
+        def add_bias(e0, e1):
+            sums = keep.tile([P, (e1 - e0) * C], F32, name="sums_%d" % e0)
+            for e in range(e0, e1):
+                cols = slice((e - e0) * C, (e - e0 + 1) * C)
+                nc.scalar.activation(sums[:, cols], acc[e][:, 0:C], IDENTITY, bias=bias[:, e : e + 1])
+            return sums
 
-        def multiply(g, h):
-            w_codes, w_scales = w_q[g, h]
-            x_codes, x_scales = x_q[g, h]
-            for i in range(GE):
-                nc.tensor.matmul_mx(
-                    out=acc[h * GE + i][:, 0:C],
-                    lhsT=w_codes[:, i * N : (i + 1) * N].bitcast(FP8X4),
-                    lhsT_scale=w_scales[:, i * N : (i + 1) * N],
-                    rhs=x_codes[:, i * C : (i + 1) * C].bitcast(FP8X4),
-                    rhs_scale=x_scales[:, i * C : (i + 1) * C],
-                    start=(g == 0),
-                    stop=(g == PASSES - 1),
-                )
+        gather(0)
+        prepare_w(0)
+        for g in range(LAST):
+            rounded = round_x(g, 0, E, "x_bf", 2)
+            gather(g + 1)
+            quantize(rounded, "x_%d" % g, x_q, [(e, g) for e in range(E)])
+            prepare_w(g + 1)
+            multiply()
 
-        sums = {}
-
-        def add_bias(h):
-            sums[h] = keep.tile([P, GS], F32, name="y_%d" % h)
-            for i in range(GE):
-                e = h * GE + i
-                nc.scalar.activation(sums[h][:, i * C : (i + 1) * C], acc[e][:, 0:C], IDENT, bias=bias[:, e : e + 1])
-
-        def scatter(h):
-            cols = offsets[:, h * GS // 16 : (h + 1) * GS // 16]
-            nc.vector.tensor_copy(window[:].indirect(cols), sums[h][:])
-
-        gather_whole(0)
-        for g in range(3):
-            for h in range(GROUPS):
-                round_w(g, h)
-            round_x_whole(g)
-            gather_whole(g + 1)
-            quantize_x_whole(g)
-            for h in range(GROUPS):
-                quantize_w(g, h)
-                multiply(g, h)
-        round_w(3, 0)
-        round_x_whole(3)
-        gather_group(4, 0)
-        round_w(4, 0)
-        round_x(4, 0)
-        quantize_x_whole(3)
-        quantize_w(3, 0)
-        multiply(3, 0)
-        gather_group(4, 1)
-        round_w(3, 1)
-        round_w(4, 1)
-        round_x(4, 1)
-        quantize_w(4, 0)
-        quantize_x(4, 0)
-        multiply(4, 0)
-        gather_group(4, 2)
-        round_w(3, 2)
-        add_bias(0)
-        round_w(4, 2)
-        round_x(4, 2)
-        quantize_w(3, 1)
-        quantize_w(4, 1)
-        quantize_x(4, 1)
-        multiply(3, 1)
-        multiply(4, 1)
-        add_bias(1)
-        scatter(0)
-        quantize_w(3, 2)
-        quantize_w(4, 2)
-        quantize_x(4, 2)
-        multiply(3, 2)
-        multiply(4, 2)
-        add_bias(2)
-        scatter(1)
-        scatter(2)
+        ahead = round_x(LAST, *GROUPS[0], "x_bf_last", len(GROUPS))
+        pending = []
+        for h, (e0, e1) in enumerate(GROUPS):
+            rounded = ahead
+            if h == 0:
+                ahead = round_x(LAST, *GROUPS[h + 1], "x_bf_last", len(GROUPS))
+            quantize(rounded, "x_last_%d" % h, x_q, [(e, LAST) for e in range(e0, e1)])
+            multiply()
+            for a, z, sums in pending:
+                nc.vector.tensor_copy(window[:].indirect(listed(a, z)), sums[:])
+            pending = [(e0 * C, e1 * C, add_bias(e0, e1))]
+            if h == 0:
+                later = round_x(LAST, *GROUPS[2], "x_bf_last", len(GROUPS))
+            elif h == 1:
+                ahead = later
+        for a, z, sums in pending:
+            nc.vector.tensor_copy(window[:].indirect(listed(a, z)), sums[:])
         nc.sync.dma_start(out=out, in_=window[:])

@@ -24,10 +24,20 @@ LAST = PASSES - 1
 PER_COLUMN = 16
 BANK = 512
 QUANT_WORDS = 512
-RUN = 2
-GROUPS = ((0, 2), (2, 4), (4, 6))
-FIRST = 256
-SPLIT = 4
+RUN = 4
+HEAD_SLOTS = 256
+X_BUFS = 14
+W_BF_BUFS = 3
+
+RANGES = ((0, 2), (2, 4), (4, 6))
+
+BATCHES = (
+    [[(e, LAST) for e in range(*RANGES[2])]]
+    + [[(e, g) for g in range(LAST)] for e in range(E)]
+    + [[(e, LAST) for e in range(RANGES[2][0])]]
+)
+WITH_PASS = [[0], [1, 2], [3, 4], [5, 6], [7]]
+HELD = E
 
 
 def tile_moe_pre_lin_bias_kernel(tc, xT, w, b, gate, offs, out):
@@ -40,22 +50,19 @@ def tile_moe_pre_lin_bias_kernel(tc, xT, w, b, gate, offs, out):
         offsets = keep.tile([P, SLOTS // PER_COLUMN], U16, name="offsets")
         gate_sb = keep.tile([P, SLOTS], F32, name="gate_sb")
         bias = keep.tile([P, E], F32, name="bias")
-        window = keep.tile([P, T], F32, name="window")
+        out_sb = keep.tile([P, T], F32, name="out_sb")
 
-        batches = [[(e, LAST) for e in range(SPLIT, E)]]
-        batches += [[(e, g) for g in range(LAST)] for e in range(E)]
-        batches += [[(e, LAST) for e in range(SPLIT)]]
         x_raw = {}
         w_raw = {}
 
         def load_x(g, t):
-            x_raw[g, t] = ring.tile([P, T], F32, name="x_raw", bufs=14)
+            x_raw[g, t] = ring.tile([P, T], F32, name="x_raw", bufs=X_BUFS)
             rows = xT[g * K_PASS : (g + 1) * K_PASS, :].rearrange("(p j) c -> p j c", j=PACK)
             nc.sync.dma_start(out=x_raw[g, t][:], in_=rows[:, t, :])
 
         def load_w(i):
-            (e0, g0), (e1, g1) = batches[i][0], batches[i][-1]
-            w_raw[i] = keep.tile([P, len(batches[i]), PACK * N], F32, name="w_raw_%d" % i)
+            (e0, g0), (e1, g1) = BATCHES[i][0], BATCHES[i][-1]
+            w_raw[i] = keep.tile([P, len(BATCHES[i]), PACK * N], F32, name="w_raw_%d" % i)
             rows = w[e0 : e1 + 1, g0 * K_PASS : (g1 + 1) * K_PASS, :]
             if e0 == e1:
                 src = rows[0].rearrange("(g p j) n -> p g (j n)", p=P, j=PACK)
@@ -63,26 +70,26 @@ def tile_moe_pre_lin_bias_kernel(tc, xT, w, b, gate, offs, out):
                 src = rows.rearrange("e (p j) n -> p e (j n)", j=PACK)
             nc.sync.dma_start(out=w_raw[i][:], in_=src)
 
-        with_pass = [[0], [1, 2], [3, 4], [5, 6], [7]]
         for g in range(PASSES):
             for t in range(PACK - 1):
                 load_x(g, t)
                 if (g, t) == (0, 0):
                     nc.sync.dma_start(offsets[:], offs)
-                    nc.sync.dma_start(out=gate_sb[:, 0:FIRST], in_=gate[0:P, 0:FIRST])
-                    nc.sync.dma_start(out=gate_sb[:, FIRST:SLOTS], in_=gate[0:P, FIRST:SLOTS])
-            for i in with_pass[g]:
+                    nc.sync.dma_start(out=gate_sb[:, 0:HEAD_SLOTS], in_=gate[0:P, 0:HEAD_SLOTS])
+                    nc.sync.dma_start(out=gate_sb[:, HEAD_SLOTS:SLOTS], in_=gate[0:P, HEAD_SLOTS:SLOTS])
+            for i in WITH_PASS[g]:
                 load_w(i)
             if g == 1:
                 nc.sync.dma_start(out=bias[:], in_=b)
             load_x(g, PACK - 1)
-        nc.vector.memset(window[:], 0.0)
+        nc.vector.memset(out_sb[:], 0.0)
 
         acc = [psum.tile([N, BANK], F32, name="acc_%d" % e) for e in range(E)]
         planes = {}
         x_q = {}
         w_q = {}
         done = set()
+        held = []
 
         def listed(a, z):
             return offsets[:, a // PER_COLUMN : z // PER_COLUMN]
@@ -91,9 +98,9 @@ def tile_moe_pre_lin_bias_kernel(tc, xT, w, b, gate, offs, out):
             planes[g] = ring.tile([P, PACK, SLOTS], F32, name="planes")
             for t in range(PACK):
                 if (g, t) == (0, 0):
-                    cuts = [(0, FIRST), (FIRST, SLOTS)]
+                    cuts = [(0, HEAD_SLOTS), (HEAD_SLOTS, SLOTS)]
                 elif (g, t) == (LAST, PACK - 1):
-                    cuts = [(e0 * C, e1 * C) for e0, e1 in GROUPS]
+                    cuts = [(e0 * C, e1 * C) for e0, e1 in RANGES]
                 else:
                     cuts = [(0, SLOTS)]
                 for a, z in cuts:
@@ -113,15 +120,16 @@ def tile_moe_pre_lin_bias_kernel(tc, xT, w, b, gate, offs, out):
             return rounded
 
         def round_w(i):
-            rounded = ring.tile([P, len(batches[i]) * N * PACK], BF16, name="w_bf", bufs=3, align_bytes=64)
-            for u in range(len(batches[i])):
+            rounded = ring.tile([P, len(BATCHES[i]) * N * PACK], BF16, name="w_bf", bufs=W_BF_BUFS, align_bytes=64)
+            for u in range(len(BATCHES[i])):
                 src = w_raw[i][:, u, :].rearrange("p (t n) -> p t n", t=PACK)
                 interleave(rounded[:, u * N * PACK : (u + 1) * N * PACK], src)
             return rounded
 
-        def quantize(rounded, name, store, keys):
+        def quantize(rounded, name, store, keys, codes=None):
             width = rounded.shape[1] // PACK
-            codes = keep.tile([P, width], U32, name=name + "_codes", align_bytes=64)
+            if codes is None:
+                codes = keep.tile([P, width], U32, name=name + "_codes", align_bytes=64)
             scales = keep.tile([P, width], U8, name=name + "_scales", align_bytes=64)
             for a in range(0, width, QUANT_WORDS):
                 z = min(a + QUANT_WORDS, width)
@@ -148,8 +156,12 @@ def tile_moe_pre_lin_bias_kernel(tc, xT, w, b, gate, offs, out):
                         done.add((e, g))
 
         def prepare_w(g):
-            for i in with_pass[g]:
-                quantize(round_w(i), "w_%d" % i, w_q, batches[i])
+            for i in WITH_PASS[g]:
+                rounded = round_w(i)
+                if i == HELD:
+                    held.append(rounded)
+                else:
+                    quantize(rounded, "w_%d" % i, w_q, BATCHES[i])
 
         def add_bias(e0, e1):
             sums = keep.tile([P, (e1 - e0) * C], F32, name="sums_%d" % e0)
@@ -157,6 +169,13 @@ def tile_moe_pre_lin_bias_kernel(tc, xT, w, b, gate, offs, out):
                 cols = slice((e - e0) * C, (e - e0 + 1) * C)
                 nc.scalar.activation(sums[:, cols], acc[e][:, 0:C], IDENTITY, bias=bias[:, e : e + 1])
             return sums
+
+        def scatter(e0, e1, sums):
+            nc.vector.tensor_copy(out_sb[:].indirect(listed(e0 * C, e1 * C)), sums[:])
+
+        def finish(e0, e1, rounded):
+            quantize(rounded, "x_last_%d" % e0, x_q, [(e, LAST) for e in range(e0, e1)])
+            multiply()
 
         gather(0)
         prepare_w(0)
@@ -167,21 +186,19 @@ def tile_moe_pre_lin_bias_kernel(tc, xT, w, b, gate, offs, out):
             prepare_w(g + 1)
             multiply()
 
-        ahead = round_x(LAST, *GROUPS[0], "x_bf_last", len(GROUPS))
-        pending = []
-        for h, (e0, e1) in enumerate(GROUPS):
-            rounded = ahead
-            if h == 0:
-                ahead = round_x(LAST, *GROUPS[h + 1], "x_bf_last", len(GROUPS))
-            quantize(rounded, "x_last_%d" % h, x_q, [(e, LAST) for e in range(e0, e1)])
-            multiply()
-            for a, z, sums in pending:
-                nc.vector.tensor_copy(window[:].indirect(listed(a, z)), sums[:])
-            pending = [(e0 * C, e1 * C, add_bias(e0, e1))]
-            if h == 0:
-                later = round_x(LAST, *GROUPS[2], "x_bf_last", len(GROUPS))
-            elif h == 1:
-                ahead = later
-        for a, z, sums in pending:
-            nc.vector.tensor_copy(window[:].indirect(listed(a, z)), sums[:])
-        nc.sync.dma_start(out=out, in_=window[:])
+        first, second, third = RANGES
+        rounded_first = round_x(LAST, *first, "shared", 1)
+        rounded_second = round_x(LAST, *second, "x_bf_last", 2)
+        finish(*first, rounded_first)
+        sums_first = add_bias(*first)
+        rounded_third = round_x(LAST, *third, "x_bf_last", 2)
+        held_codes = ring.tile([P, LAST * N], U32, name="shared", bufs=1, align_bytes=64)
+        quantize(held[0], "w_held", w_q, BATCHES[HELD], held_codes)
+        finish(*second, rounded_second)
+        sums_second = add_bias(*second)
+        scatter(*first, sums_first)
+        finish(*third, rounded_third)
+        sums_third = add_bias(*third)
+        scatter(*second, sums_second)
+        scatter(*third, sums_third)
+        nc.sync.dma_start(out=out, in_=out_sb[:])

from contextlib import ExitStack

import concourse.mybir as mybir

K, T, E, C, N = 2560, 1024, 6, 128, 128
SLOTS = E * C
P = 128
FLOPS = 2 * K * N * SLOTS
BYTES = 4 * (K * T + E * K * N + N * E + P * SLOTS + N * T) + 2 * P * (SLOTS // 16)

F32 = mybir.dt.float32
BF16 = mybir.dt.bfloat16
U32 = mybir.dt.uint32
U16 = mybir.dt.uint16
U8 = mybir.dt.uint8
FP8X4 = mybir.dt.float8_e4m3fn_x4
MULT = mybir.AluOpType.mult
IDENTITY = mybir.ActivationFunctionType.Identity

PACK = 4
K_PASS = P * PACK
PASSES = K // K_PASS
LAST = PASSES - 1
PER_COLUMN = 16
BANK = 512
QUANT_WORDS = 512
RUN = 4
HEAD_SLOTS = 256
X_BUFS = 14
W_BF_BUFS = 3

RANGES = ((0, 2), (2, 4), (4, 6))

BATCHES = (
    [[(e, LAST) for e in range(*RANGES[2])]]
    + [[(e, g) for g in range(LAST)] for e in range(E)]
    + [[(e, LAST) for e in range(RANGES[2][0])]]
)
WITH_PASS = [[0], [1, 2], [3, 4], [5, 6], [7]]
HELD = E


def tile_moe_pre_lin_bias_kernel(tc, xT, w, b, gate, offs, out):
    nc = tc.nc
    with ExitStack() as ctx:
        keep = ctx.enter_context(tc.tile_pool(name="keep", bufs=1))
        ring = ctx.enter_context(tc.tile_pool(name="ring", bufs=2))
        psum = ctx.enter_context(tc.psum_pool(name="psum", bufs=1))

        offsets = keep.tile([P, SLOTS // PER_COLUMN], U16, name="offsets")
        gate_sb = keep.tile([P, SLOTS], F32, name="gate_sb")
        bias = keep.tile([P, E], F32, name="bias")
        out_sb = keep.tile([P, T], F32, name="out_sb")

        x_raw = {}
        w_raw = {}

        def load_x(g, t):
            x_raw[g, t] = ring.tile([P, T], F32, name="x_raw", bufs=X_BUFS)
            rows = xT[g * K_PASS : (g + 1) * K_PASS, :].rearrange("(p j) c -> p j c", j=PACK)
            nc.sync.dma_start(out=x_raw[g, t][:], in_=rows[:, t, :])

        def load_w(i):
            (e0, g0), (e1, g1) = BATCHES[i][0], BATCHES[i][-1]
            w_raw[i] = keep.tile([P, len(BATCHES[i]), PACK * N], F32, name="w_raw_%d" % i)
            rows = w[e0 : e1 + 1, g0 * K_PASS : (g1 + 1) * K_PASS, :]
            if e0 == e1:
                src = rows[0].rearrange("(g p j) n -> p g (j n)", p=P, j=PACK)
            else:
                src = rows.rearrange("e (p j) n -> p e (j n)", j=PACK)
            nc.sync.dma_start(out=w_raw[i][:], in_=src)

        for g in range(PASSES):
            for t in range(PACK - 1):
                load_x(g, t)
                if (g, t) == (0, 0):
                    nc.sync.dma_start(offsets[:], offs)
                    nc.sync.dma_start(out=gate_sb[:, 0:HEAD_SLOTS], in_=gate[0:P, 0:HEAD_SLOTS])
                    nc.sync.dma_start(out=gate_sb[:, HEAD_SLOTS:SLOTS], in_=gate[0:P, HEAD_SLOTS:SLOTS])
            for i in WITH_PASS[g]:
                load_w(i)
            if g == 1:
                nc.sync.dma_start(out=bias[:], in_=b)
            load_x(g, PACK - 1)
        nc.vector.memset(out_sb[:], 0.0)

        acc = [psum.tile([N, BANK], F32, name="acc_%d" % e) for e in range(E)]
        planes = {}
        x_q = {}
        w_q = {}
        done = set()
        held = []

        def listed(a, z):
            return offsets[:, a // PER_COLUMN : z // PER_COLUMN]

        def gather(g):
            planes[g] = ring.tile([P, PACK, SLOTS], F32, name="planes")
            for t in range(PACK):
                if (g, t) == (0, 0):
                    cuts = [(0, HEAD_SLOTS), (HEAD_SLOTS, SLOTS)]
                elif (g, t) == (LAST, PACK - 1):
                    cuts = [(e0 * C, e1 * C) for e0, e1 in RANGES]
                else:
                    cuts = [(0, SLOTS)]
                for a, z in cuts:
                    nc.vector.tensor_tensor(
                        planes[g][:, t, a:z], x_raw[g, t][:].indirect(listed(a, z)), gate_sb[:, a:z], MULT
                    )

        def interleave(dst, src):
            nc.scalar.copy(
                out=dst.rearrange("p (c i t) -> p c t i", i=RUN, t=PACK),
                in_=src.rearrange("p t (c i) -> p c t i", i=RUN),
            )

        def round_x(g, e0, e1, tag, bufs):
            rounded = ring.tile([P, (e1 - e0) * C * PACK], BF16, name=tag, bufs=bufs, align_bytes=64)
            interleave(rounded[:], planes[g][:, :, e0 * C : e1 * C])
            return rounded

        def round_w(i):
            rounded = ring.tile([P, len(BATCHES[i]) * N * PACK], BF16, name="w_bf", bufs=W_BF_BUFS, align_bytes=64)
            for u in range(len(BATCHES[i])):
                src = w_raw[i][:, u, :].rearrange("p (t n) -> p t n", t=PACK)
                interleave(rounded[:, u * N * PACK : (u + 1) * N * PACK], src)
            return rounded

        def quantize(rounded, name, store, keys, codes=None):
            width = rounded.shape[1] // PACK
            if codes is None:
                codes = keep.tile([P, width], U32, name=name + "_codes", align_bytes=64)
            scales = keep.tile([P, width], U8, name=name + "_scales", align_bytes=64)
            for a in range(0, width, QUANT_WORDS):
                z = min(a + QUANT_WORDS, width)
                nc.vector.quantize_mx(
                    out=codes[:, a:z].bitcast(FP8X4), scales=scales[:, a:z], in_=rounded[:, a * PACK : z * PACK]
                )
            for u, key in enumerate(keys):
                store[key] = codes[:, u * P : (u + 1) * P].bitcast(FP8X4), scales[:, u * P : (u + 1) * P]

        def multiply():
            for g in range(PASSES):
                for e in range(E):
                    ready = (e, g) in x_q and (e, g) in w_q and (g == 0 or (e, g - 1) in done)
                    if ready and (e, g) not in done:
                        nc.tensor.matmul_mx(
                            out=acc[e][:, 0:C],
                            lhsT=w_q[e, g][0],
                            lhsT_scale=w_q[e, g][1],
                            rhs=x_q[e, g][0],
                            rhs_scale=x_q[e, g][1],
                            start=(g == 0),
                            stop=(g == LAST),
                        )
                        done.add((e, g))

        def prepare_w(g):
            for i in WITH_PASS[g]:
                rounded = round_w(i)
                if i == HELD:
                    held.append(rounded)
                else:
                    quantize(rounded, "w_%d" % i, w_q, BATCHES[i])

        def add_bias(e0, e1):
            sums = keep.tile([P, (e1 - e0) * C], F32, name="sums_%d" % e0)
            for e in range(e0, e1):
                cols = slice((e - e0) * C, (e - e0 + 1) * C)
                nc.scalar.activation(sums[:, cols], acc[e][:, 0:C], IDENTITY, bias=bias[:, e : e + 1])
            return sums

        def scatter(e0, e1, sums):
            nc.vector.tensor_copy(out_sb[:].indirect(listed(e0 * C, e1 * C)), sums[:])

        def finish(e0, e1, rounded):
            quantize(rounded, "x_last_%d" % e0, x_q, [(e, LAST) for e in range(e0, e1)])
            multiply()

        gather(0)
        prepare_w(0)
        for g in range(LAST):
            rounded = round_x(g, 0, E, "x_bf", 2)
            gather(g + 1)
            quantize(rounded, "x_%d" % g, x_q, [(e, g) for e in range(E)])
            prepare_w(g + 1)
            multiply()

        first, second, third = RANGES
        rounded_first = round_x(LAST, *first, "shared", 1)
        rounded_second = round_x(LAST, *second, "x_bf_last", 2)
        finish(*first, rounded_first)
        sums_first = add_bias(*first)
        rounded_third = round_x(LAST, *third, "x_bf_last", 2)
        held_codes = ring.tile([P, LAST * N], U32, name="shared", bufs=1, align_bytes=64)
        quantize(held[0], "w_held", w_q, BATCHES[HELD], held_codes)
        finish(*second, rounded_second)
        sums_second = add_bias(*second)
        scatter(*first, sums_first)
        finish(*third, rounded_third)
        sums_third = add_bias(*third)
        scatter(*second, sums_second)
        scatter(*third, sums_third)
        nc.sync.dma_start(out=out, in_=out_sb[:])
